import numpy as np
import ml_dtypes


def mxq(x, axis, fmt="e4m3"):
    dtype, down = {"e4m3": (ml_dtypes.float8_e4m3fn, 7), "e5m2": (ml_dtypes.float8_e5m2, 14)}[fmt]
    v = np.moveaxis(np.asarray(x, np.float32).astype(ml_dtypes.bfloat16).astype(np.float64), axis, -1)
    blocks = v.reshape(v.shape[:-1] + (-1, 32))
    amax = np.abs(blocks).max(-1, keepdims=True)
    byte = np.maximum(np.where(amax > 0, np.frexp(amax)[1] - 1 + 127, 0) - down, 1)
    scale = np.exp2(byte - 127.0)
    codes = (blocks / scale).astype(np.float32).astype(dtype).astype(np.float64)
    return np.moveaxis((codes * scale).reshape(v.shape), -1, axis)


WIDE = False


def mx_kscale(k):
    if not WIDE:
        return np.ones(k)
    levels = np.array([30, -30])
    if k % 512:
        return np.exp2(np.random.permutation(np.resize(levels, k // 32))).repeat(32)
    a = np.empty((k // 512, 16))
    for p in range(k // 512):
        a[p, :8] = np.random.permutation(np.resize(levels, 8))
        for g in range(8):
            far = levels[np.abs(levels - a[p, g]) >= 10]
            a[p, g + 8] = far[np.random.randint(len(far))]
    return np.exp2(a.ravel()).repeat(32)


BF16 = ml_dtypes.bfloat16


def bf(x):
    return np.asarray(x, np.float32).astype(BF16)


def f64(x):
    return np.asarray(x).astype(np.float64)


M, K, N, R = 1024, 1024, 2048, 1024


def setup_inputs():
    s = mx_kscale(K)
    t = mx_kscale(N)
    x = np.random.standard_normal((M, K))
    down = np.random.standard_normal((K, R)) / np.sqrt(K)
    dy = np.random.standard_normal((M, N)) * np.exp(0.7 * np.random.standard_normal((M, N)))
    up = np.random.standard_normal((R, N)) / np.sqrt(N)
    return {"x": bf(x * s),
            "down": bf(down / s[:, None]),
            "dy": bf(dy * t),
            "up": bf(up / t),
            "gate": bf(np.random.uniform(0.2, 1.8, (M, R))),
            "centre": bf(0.3 * np.random.standard_normal(R))}


def reference(x, down, dy, up, gate, centre):
    xq = mxq(f64(x), 1, "e4m3")
    downq = mxq(f64(down), 0, "e4m3")
    dyq = mxq(f64(dy), 1, "e5m2")
    upq = mxq(f64(up), 1, "e4m3")
    total = (xq @ downq) + (dyq @ upq.T)
    return f64(gate) * (total - f64(centre))

@@ -1,0 +1,305 @@
+from contextlib import ExitStack
+
+import concourse.mybir as mybir
+from concourse.masks import make_identity
+
+TOKENS, FEATURES, OUT_FEATURES, RANKS = 1024, 1024, 2048, 1024
+FLOPS = 2 * TOKENS * RANKS * (FEATURES + OUT_FEATURES)
+
+F32 = mybir.dt.float32
+BF16 = mybir.dt.bfloat16
+U32 = mybir.dt.uint32
+U8 = mybir.dt.uint8
+E4M3 = mybir.dt.float8_e4m3fn_x4
+E5M2 = mybir.dt.float8_e5m2_x4
+SUB = mybir.AluOpType.subtract
+MULT = mybir.AluOpType.mult
+
+P = 128
+HALF = 512
+
+REORDER_HEAD = ("v", "v", None, None)
+REORDER_LATE = ("v", "v", None, None)
+DOWN_ENGINE = {"dnA0": "v", "dnA1": "v", "dnB0": "s", "dnB1": "s"}
+
+
+def tile_stacked_lora_rank_grad_s2_kernel(tc, x, down, dy, up, gate, centre, out):
+    nc = tc.nc
+    with ExitStack() as ctx:
+        const = ctx.enter_context(tc.tile_pool(name="const", bufs=1))
+        rawp = ctx.enter_context(tc.tile_pool(name="rawp", bufs=18))
+        rop = ctx.enter_context(tc.tile_pool(name="rop", bufs=8))
+        grpp = ctx.enter_context(tc.tile_pool(name="grpp", bufs=4))
+        keep = ctx.enter_context(tc.tile_pool(name="keep", bufs=1))
+        resp = ctx.enter_context(tc.tile_pool(name="resp", bufs=12))
+        psum = ctx.enter_context(tc.psum_pool(name="psum", bufs=1))
+        ctx.enter_context(tc.manual_schedule())
+
+        raw, codes, scales, grp, ro, bank = {}, {}, {}, {}, {}, {}
+        acc, res = {}, {}
+        gates = {}
+
+        def load_cols(name, src, r0, c, split=1):
+            t = rawp.tile([P, 2048], BF16, tag="raw", name="raw_" + name, align_bytes=64)
+            v = t[:].rearrange("p (a k) -> p a k", a=4)
+            s = src[r0 : r0 + HALF, c * 512 : (c + 1) * 512].rearrange("(a p) k -> p a k", p=P)
+            n = 4 // split
+            for h in range(split):
+                nc.sync.dma_start(out=v[:, h * n : (h + 1) * n, :], in_=s[:, h * n : (h + 1) * n, :])
+            raw[name] = t
+
+        def load_tokens(name, src, r0, k0):
+            t = rawp.tile([P, 2048], BF16, tag="raw", name="raw_" + name, align_bytes=64)
+            nc.sync.dma_start(
+                out=t[:].rearrange("p (a k) -> p a k", a=2),
+                in_=src[r0 : r0 + 256, k0 : k0 + 1024].rearrange("(a p) k -> p a k", p=P),
+            )
+            raw[name] = t
+
+        def load_down(name, c, w):
+            t = rawp.tile([P, 2048], BF16, tag="raw", name="raw_" + name, align_bytes=64)
+            nc.sync.dma_start(
+                out=t[:].rearrange("p (j r) -> p j r", j=4),
+                in_=down[c * 512 : (c + 1) * 512, w * HALF : (w + 1) * HALF].rearrange("(p j) r -> p j r", j=4),
+            )
+            raw[name] = t
+
+        def load_gate(g):
+            t = const.tile([P, 4, RANKS], BF16, name="gate_%d" % g)
+            nc.sync.dma_start(out=t[:], in_=gate[g * HALF : (g + 1) * HALF, :].rearrange("(a p) r -> p a r", p=P))
+            gates[g] = t
+
+        crow = const.tile([P, P], BF16, name="crow")
+        nc.vector.memset(crow[:], 0.0)
+        nc.scalar.dma_start(out=crow[0:8, :], in_=centre.rearrange("(m p) -> m p", p=P))
+        dummy = const.tile([P, 8], F32, name="dummy")
+        nc.vector.memset(dummy[:], 0.0)
+        dummy2 = const.tile([P, 8], F32, name="dummy2")
+        nc.scalar.copy(out=dummy2[:], in_=dummy[:])
+        ident = const.tile([P, P], F32, name="ident")
+        make_identity(nc, ident[:])
+
+        load_cols("dyA0", dy, 0, 0, split=2)
+        load_cols("upA0", up, 0, 0, split=2)
+        for c in (1, 2, 3):
+            load_cols("dyA%d" % c, dy, 0, c)
+            load_cols("upA%d" % c, up, 0, c)
+        load_tokens("x01", x, 0, 0)
+        load_tokens("x23", x, 256, 0)
+        load_down("dnA0", 0, 0)
+        load_down("dnA1", 1, 0)
+        for c in range(4):
+            load_cols("upB%d" % c, up, HALF, c)
+        load_down("dnB0", 0, 1)
+        load_down("dnB1", 1, 1)
+
+        crow32 = const.tile([P, P], F32, name="crow32")
+        c8 = const.tile([P, 8], F32, name="c8")
+        cb = const.tile([P, RANKS], F32, name="cb")
+
+        def centre_columns():
+            nc.vector.tensor_copy(out=crow32[:], in_=crow[:])
+            t = psum.tile([P, HALF], F32, tag="acc0", name="ctr")
+            nc.tensor.transpose(t[:, 0:P], crow32[:], ident[:])
+            nc.scalar.copy(out=c8[:], in_=t[:, 0:8])
+
+        def centre_spread():
+            for h in range(2):
+                t = psum.tile([P, HALF], F32, tag="acc%d" % (1 + h), name="ctrb%d" % h)
+                for m in range(4):
+                    col = 4 * h + m
+                    nc.tensor.transpose(t[:, m * P : (m + 1) * P], c8[:, col : col + 1].to_broadcast([P, P]), ident[:])
+                nc.scalar.copy(out=cb[:, h * HALF : (h + 1) * HALF], in_=t[:])
+
+        pairs = [
+            ("dyA0", "upA0"), ("dyA1", "upA1"), ("dyA2", "upA2"), ("dyA3", "upA3"), ("x01", "x23"),
+            ("upB0", "upB1"), ("upB2", "upB3"), ("dy45a", "dy45b"), ("x45", "dy67a"), ("dy67b", "x67"),
+        ]
+
+        def route(i, j):
+            if i == 0:
+                return None
+            return (REORDER_HEAD if i < 5 else REORDER_LATE)[j]
+
+        def words(i, j):
+            return raw[pairs[i][j // 2]][:, (j % 2) * 1024 : (j % 2 + 1) * 1024].bitcast(F32)
+
+        def R(i, j):
+            if i > 9 or route(i, j) is None:
+                return
+            t = rop.tile([P, 512], F32, tag="ro", name="ro_%d_%d" % (i, j))
+            o = t[:].rearrange("p (g u m) -> p g u m", g=2, u=2)
+            s = words(i, j).rearrange("p (g m u) -> p g u m", g=2, u=2)
+            if route(i, j) == "v":
+                nc.vector.tensor_copy(out=o, in_=s)
+            else:
+                nc.scalar.copy(out=o, in_=s)
+            ro[i, j] = t
+
+        def T(i, j):
+            b = psum.tile([P, 512], F32, tag="t%d" % j, name="tb_%d_%d" % (i, j))
+            w = words(i, j)
+            for g in range(2):
+                for u in range(2):
+                    q = 2 * g + u
+                    src = ro[i, j][:, q * P : (q + 1) * P] if (i, j) in ro else w[:, 256 * g + u : 256 * (g + 1) : 2]
+                    nc.tensor.transpose(b[:, q * P : (q + 1) * P], src, ident[:])
+            bank[i, j] = b
+
+        def E(i, j):
+            name = pairs[i][j // 2]
+            if j % 2 == 0:
+                grp[name] = grpp.tile([P, 2048], BF16, tag="grp", name="grp_" + name, align_bytes=64)
+            o = grp[name][:, (j % 2) * 1024 : (j % 2 + 1) * 1024].bitcast(F32).rearrange("p (g r u) -> p g r u", g=2, u=2)
+            nc.scalar.copy(out=o, in_=bank[i, j][:].rearrange("p (g u r) -> p g r u", g=2, u=2))
+
+        def quantize(name, fmt):
+            codes[name] = keep.tile([P, 512], U32, name="codes_" + name, align_bytes=64)
+            scales[name] = keep.tile([P, 512], U8, name="scales_" + name, align_bytes=64)
+            nc.vector.quantize_mx(out=codes[name][:].bitcast(fmt), scales=scales[name][:], in_=grp[name][:])
+
+        def Q(i, p):
+            name = pairs[i][p]
+            quantize(name, E5M2 if name[0] == "d" else E4M3)
+
+        def DI(name):
+            grp[name] = grpp.tile([P, 2048], BF16, tag="grp", name="grp_" + name, align_bytes=64)
+            o = grp[name][:].rearrange("p (r j) -> p r j", j=4)
+            s = raw[name][:].rearrange("p (j r) -> p r j", j=4)
+            if DOWN_ENGINE[name] == "v":
+                nc.vector.tensor_copy(out=o, in_=s)
+            else:
+                nc.scalar.copy(out=o, in_=s)
+
+        def DQ(name):
+            quantize(name, E4M3)
+
+        def M(b, tok, q, rank, start, stop):
+            if start:
+                acc[b] = psum.tile([P, HALF], F32, tag="acc%d" % b, name="acc_%d" % b)
+            cols = slice(q * P, (q + 1) * P)
+            nc.tensor.matmul_mx(
+                out=acc[b][:],
+                lhsT=codes[tok][:, cols].bitcast(E5M2 if tok[0] == "d" else E4M3),
+                lhsT_scale=scales[tok][:, cols],
+                rhs=codes[rank][:].bitcast(E4M3),
+                rhs_scale=scales[rank][:],
+                start=start,
+                stop=stop,
+            )
+
+        def O1(b, tile, w):
+            t = resp.tile([P, HALF], F32, tag="res", name="res_%d_%d" % (tile, w))
+            nc.vector.tensor_tensor(out=t[:], in0=acc[b][:], in1=cb[:, w * HALF : (w + 1) * HALF], op=SUB)
+            res[tile, w] = t
+
+        def O2(tile, w):
+            t = res[tile, w]
+            g = gates[tile // 4][:, tile % 4, w * HALF : (w + 1) * HALF]
+            nc.vector.tensor_tensor(out=t[:], in0=t[:], in1=g, op=MULT)
+            nc.sync.dma_start(out=out[tile * P : (tile + 1) * P, w * HALF : (w + 1) * HALF], in_=t[:])
+
+        def xq(b):
+            return ("x01" if b < 2 else "x23"), 2 * (b % 2)
+
+        def token_tile(base, a, parts, first, last):
+            for w in (0, 1):
+                for n, tok in enumerate(parts):
+                    kind = tok[-1] if tok[0] == "d" else "x"
+                    for c in (0, 1):
+                        rank = ("dn%s%d" % ("AB"[w], c)) if kind == "x" else ("up%s%d" % ("AB"[w], c + (2 if kind == "b" else 0)))
+                        M(base + w, tok, 2 * a + c, rank, first and n == 0 and c == 0, last and n == len(parts) - 1 and c == 1)
+
+        def products(i):
+            if 1 <= i <= 4:
+                for b in range(4):
+                    M(b, "dyA%d" % (i - 1), b, "upA%d" % (i - 1), i == 1, False)
+            elif i == 5:
+                for b in range(4):
+                    tok, q = xq(b)
+                    for c in (0, 1):
+                        M(b, tok, q + c, "dnA%d" % c, False, c == 1)
+            elif i == 6:
+                for c in (0, 1):
+                    for b in range(4):
+                        M(b, "dyA%d" % c, b, "upB%d" % c, c == 0, False)
+            elif i == 7:
+                for b in range(4):
+                    for c in (2, 3):
+                        M(b, "dyA%d" % c, b, "upB%d" % c, False, False)
+                    tok, q = xq(b)
+                    for c in (0, 1):
+                        M(b, tok, q + c, "dnB%d" % c, False, c == 1)
+            elif i == 8:
+                token_tile(0, 0, ["dy45a", "dy45b"], True, False)
+            elif i == 9:
+                token_tile(0, 0, ["x45"], False, True)
+                token_tile(2, 1, ["dy45a", "dy45b", "x45"], True, True)
+
+        for j in range(4):
+            R(0, j)
+        for i in range(10):
+            for j in range(4):
+                T(i, j)
+            if i == 6:
+                for b in range(4):
+                    O1(b, b, 0)
+            if i == 8:
+                for b in range(4):
+                    O1(b, b, 1)
+            if i == 0:
+                centre_columns()
+            E(i, 0)
+            R(i + 1, 0)
+            R(i + 1, 1)
+            E(i, 1)
+            Q(i, 0)
+            E(i, 2)
+            R(i + 1, 2)
+            R(i + 1, 3)
+            E(i, 3)
+            Q(i, 1)
+            if i == 0:
+                centre_spread()
+            if i == 3:
+                DI("dnA0")
+            if i == 4:
+                DQ("dnA0")
+                DI("dnA1")
+                DQ("dnA1")
+            if i == 5:
+                DI("dnB0")
+            if i == 6:
+                DI("dnB1")
+                DQ("dnB0")
+                DQ("dnB1")
+            if i == 7:
+                for b in range(4):
+                    O2(b, 0)
+            if i == 8:
+                for b in range(4):
+                    O2(b, 1)
+            products(i)
+            if i == 0:
+                load_tokens("dy45a", dy, 512, 0)
+                load_tokens("dy45b", dy, 512, 1024)
+                load_gate(0)
+            if i == 1:
+                load_tokens("x45", x, 512, 0)
+                load_tokens("dy67a", dy, 768, 0)
+            if i == 2:
+                load_tokens("dy67b", dy, 768, 1024)
+                load_tokens("x67", x, 768, 0)
+                load_gate(1)
+            if i == 9:
+                for tile, b in ((4, 0), (5, 2)):
+                    O1(b, tile, 0)
+                    O1(b + 1, tile, 1)
+                    O2(tile, 0)
+                    O2(tile, 1)
+        for tile, b in ((6, 0), (7, 2)):
+            token_tile(b, tile - 6, ["dy67a", "dy67b", "x67"], True, True)
+            O1(b, tile, 0)
+            O1(b + 1, tile, 1)
+            O2(tile, 0)
+            O2(tile, 1)

@@ -18,9 +18,49 @@ MULT = mybir.AluOpType.mult
 P = 128
 HALF = 512
 
-REORDER_HEAD = ("v", "v", None, None)
-REORDER_LATE = ("v", "v", None, None)
-DOWN_ENGINE = {"dnA0": "v", "dnA1": "v", "dnB0": "s", "dnB1": "s"}
+PASSES_AFTER = (0, 0, 0, 0, 0, 0, 4, 0, 2, 6, 4, 6, 4, 6, 0, 10, 0, 16, 0, 4)
+PLAIN_PAIRS = 7
+VECTOR_PAIRS = 11
+DOWN_HALVES = {"dnA0": (7, 7), "dnA1": (7, 9), "dnB0": (13, 13), "dnB1": (12, 13)}
+
+
+PAIRS = (
+    "dyA0", "upA0", "dyA1", "upA1", "dyA2", "upA2", "dyA3", "upA3", "x01", "x23",
+    "upB0", "upB1", "upB2", "upB3", "dy45a", "dy45b", "x45", "dy67a", "dy67b", "x67",
+)
+
+
+def pass_list():
+    o = []
+
+    def group_a(w, cs, first):
+        h = "AB"[w]
+        for c in cs:
+            for b in range(4):
+                o.append((b, "dyA%d" % c, b, "up%s%d" % (h, c), first and c == 0, False, b, w))
+
+    def x_part(w, b):
+        for c in (0, 1):
+            o.append((b, "x01" if b < 2 else "x23", 2 * (b % 2) + c, "dn%s%d" % ("AB"[w], c), False, c == 1, b, w))
+
+    group_a(0, range(4), True)
+    for b in range(4):
+        x_part(0, b)
+    group_a(1, range(2), True)
+    for b in range(4):
+        for c in (2, 3):
+            o.append((b, "dyA%d" % c, b, "upB%d" % c, False, False, b, 1))
+        x_part(1, b)
+    for t in range(4, 8):
+        g = "45" if t < 6 else "67"
+        a = t % 2
+        for w in (0, 1):
+            h = "AB"[w]
+            for c in range(6):
+                tok = ("dy%s%s" % (g, "ab"[c // 2])) if c < 4 else "x" + g
+                rank = ("up%s%d" % (h, c)) if c < 4 else ("dn%s%d" % (h, c - 4))
+                o.append((2 * a + w, tok, 2 * a + c % 2, rank, c == 0, c == 5, t, w))
+    return o
 
 
 def tile_stacked_lora_rank_grad_s2_kernel(tc, x, down, dy, up, gate, centre, out):
@@ -29,15 +69,15 @@ def tile_stacked_lora_rank_grad_s2_kernel(tc, x, down, dy, up, gate, centre, out
         const = ctx.enter_context(tc.tile_pool(name="const", bufs=1))
         rawp = ctx.enter_context(tc.tile_pool(name="rawp", bufs=18))
         rop = ctx.enter_context(tc.tile_pool(name="rop", bufs=8))
-        grpp = ctx.enter_context(tc.tile_pool(name="grpp", bufs=4))
+        grpp = ctx.enter_context(tc.tile_pool(name="grpp", bufs=3))
+        dnp = ctx.enter_context(tc.tile_pool(name="dnp", bufs=2))
         keep = ctx.enter_context(tc.tile_pool(name="keep", bufs=1))
         resp = ctx.enter_context(tc.tile_pool(name="resp", bufs=12))
         psum = ctx.enter_context(tc.psum_pool(name="psum", bufs=1))
         ctx.enter_context(tc.manual_schedule())
 
         raw, codes, scales, grp, ro, bank = {}, {}, {}, {}, {}, {}
-        acc, res = {}, {}
-        gates = {}
+        acc, res, gates = {}, {}, {}
 
         def load_cols(name, src, r0, c, split=1):
             t = rawp.tile([P, 2048], BF16, tag="raw", name="raw_" + name, align_bytes=64)
@@ -69,15 +109,18 @@ def tile_stacked_lora_rank_grad_s2_kernel(tc, x, down, dy, up, gate, centre, out
             nc.sync.dma_start(out=t[:], in_=gate[g * HALF : (g + 1) * HALF, :].rearrange("(a p) r -> p a r", p=P))
             gates[g] = t
 
-        crow = const.tile([P, P], BF16, name="crow")
+        crow = const.tile([P, P], F32, name="crow", align_bytes=64)
         nc.vector.memset(crow[:], 0.0)
-        nc.scalar.dma_start(out=crow[0:8, :], in_=centre.rearrange("(m p) -> m p", p=P))
+        nc.scalar.dma_start(out=crow[0:4, :].bitcast(BF16), in_=centre.rearrange("(m q) -> m q", m=4))
         dummy = const.tile([P, 8], F32, name="dummy")
         nc.vector.memset(dummy[:], 0.0)
         dummy2 = const.tile([P, 8], F32, name="dummy2")
         nc.scalar.copy(out=dummy2[:], in_=dummy[:])
-        ident = const.tile([P, P], F32, name="ident")
+        ident = const.tile([P, P], F32, name="ident", align_bytes=64)
         make_identity(nc, ident[:])
+        c4 = const.tile([P, 4], F32, name="c4")
+        cbw = const.tile([P, HALF], F32, name="cbw", align_bytes=64)
+        cb = cbw[:].bitcast(BF16)
 
         load_cols("dyA0", dy, 0, 0, split=2)
         load_cols("upA0", up, 0, 0, split=2)
@@ -93,86 +136,73 @@ def tile_stacked_lora_rank_grad_s2_kernel(tc, x, down, dy, up, gate, centre, out
         load_down("dnB0", 0, 1)
         load_down("dnB1", 1, 1)
 
-        crow32 = const.tile([P, P], F32, name="crow32")
-        c8 = const.tile([P, 8], F32, name="c8")
-        cb = const.tile([P, RANKS], F32, name="cb")
+        def late_loads():
+            load_tokens("dy45a", dy, 512, 0)
+            load_tokens("dy45b", dy, 512, 1024)
+            load_gate(0)
+            load_tokens("x45", x, 512, 0)
+            load_tokens("dy67a", dy, 768, 0)
+            load_tokens("dy67b", dy, 768, 1024)
+            load_tokens("x67", x, 768, 0)
+            load_gate(1)
 
         def centre_columns():
-            nc.vector.tensor_copy(out=crow32[:], in_=crow[:])
             t = psum.tile([P, HALF], F32, tag="acc0", name="ctr")
-            nc.tensor.transpose(t[:, 0:P], crow32[:], ident[:])
-            nc.scalar.copy(out=c8[:], in_=t[:, 0:8])
+            nc.tensor.transpose(t[:, 0:P], crow[:], ident[:])
+            nc.vector.tensor_copy(out=c4[:], in_=t[:, 0:4])
 
         def centre_spread():
-            for h in range(2):
-                t = psum.tile([P, HALF], F32, tag="acc%d" % (1 + h), name="ctrb%d" % h)
-                for m in range(4):
-                    col = 4 * h + m
-                    nc.tensor.transpose(t[:, m * P : (m + 1) * P], c8[:, col : col + 1].to_broadcast([P, P]), ident[:])
-                nc.scalar.copy(out=cb[:, h * HALF : (h + 1) * HALF], in_=t[:])
+            t = psum.tile([P, HALF], F32, tag="acc1", name="ctrb")
+            for m in range(4):
+                nc.tensor.transpose(t[:, m * P : (m + 1) * P], c4[:, m : m + 1].to_broadcast([P, P]), ident[:])
+            nc.vector.tensor_copy(out=cbw[:], in_=t[:])
 
-        pairs = [
-            ("dyA0", "upA0"), ("dyA1", "upA1"), ("dyA2", "upA2"), ("dyA3", "upA3"), ("x01", "x23"),
-            ("upB0", "upB1"), ("upB2", "upB3"), ("dy45a", "dy45b"), ("x45", "dy67a"), ("dy67b", "x67"),
-        ]
+        def words(p, j):
+            return raw[PAIRS[p]][:, j * 1024 : (j + 1) * 1024].bitcast(F32)
 
-        def route(i, j):
-            if i == 0:
-                return None
-            return (REORDER_HEAD if i < 5 else REORDER_LATE)[j]
+        def R(p):
+            for j in (0, 1):
+                t = rop.tile([P, 512], F32, tag="ro", name="ro_%d_%d" % (p, j), align_bytes=64)
+                o = t[:].rearrange("p (g u m) -> p g u m", g=2, u=2)
+                s = words(p, j).rearrange("p (g m u) -> p g u m", g=2, u=2)
+                if p < VECTOR_PAIRS:
+                    nc.vector.tensor_copy(out=o, in_=s)
+                else:
+                    nc.scalar.copy(out=o, in_=s)
+                ro[p, j] = t
 
-        def words(i, j):
-            return raw[pairs[i][j // 2]][:, (j % 2) * 1024 : (j % 2 + 1) * 1024].bitcast(F32)
-
-        def R(i, j):
-            if i > 9 or route(i, j) is None:
-                return
-            t = rop.tile([P, 512], F32, tag="ro", name="ro_%d_%d" % (i, j))
-            o = t[:].rearrange("p (g u m) -> p g u m", g=2, u=2)
-            s = words(i, j).rearrange("p (g m u) -> p g u m", g=2, u=2)
-            if route(i, j) == "v":
-                nc.vector.tensor_copy(out=o, in_=s)
-            else:
-                nc.scalar.copy(out=o, in_=s)
-            ro[i, j] = t
-
-        def T(i, j):
-            b = psum.tile([P, 512], F32, tag="t%d" % j, name="tb_%d_%d" % (i, j))
-            w = words(i, j)
+        def T(p, j):
+            b = psum.tile([P, 512], F32, tag="t%d" % (2 * (p % 2) + j), name="tb_%d_%d" % (p, j))
             for g in range(2):
                 for u in range(2):
                     q = 2 * g + u
-                    src = ro[i, j][:, q * P : (q + 1) * P] if (i, j) in ro else w[:, 256 * g + u : 256 * (g + 1) : 2]
+                    if p < PLAIN_PAIRS:
+                        src = words(p, j)[:, 256 * g + u : 256 * (g + 1) : 2]
+                    else:
+                        src = ro[p, j][:, q * P : (q + 1) * P]
                     nc.tensor.transpose(b[:, q * P : (q + 1) * P], src, ident[:])
-            bank[i, j] = b
+            bank[p, j] = b
 
-        def E(i, j):
-            name = pairs[i][j // 2]
-            if j % 2 == 0:
+        def E(p, j):
+            name = PAIRS[p]
+            if j == 0:
                 grp[name] = grpp.tile([P, 2048], BF16, tag="grp", name="grp_" + name, align_bytes=64)
-            o = grp[name][:, (j % 2) * 1024 : (j % 2 + 1) * 1024].bitcast(F32).rearrange("p (g r u) -> p g r u", g=2, u=2)
-            nc.scalar.copy(out=o, in_=bank[i, j][:].rearrange("p (g u r) -> p g r u", g=2, u=2))
+            o = grp[name][:, j * 1024 : (j + 1) * 1024].bitcast(F32).rearrange("p (g r u) -> p g r u", g=2, u=2)
+            nc.scalar.copy(out=o, in_=bank[p, j][:].rearrange("p (g u r) -> p g r u", g=2, u=2))
 
-        def quantize(name, fmt):
+        def Q(name):
+            fmt = E5M2 if name[0:2] == "dy" else E4M3
             codes[name] = keep.tile([P, 512], U32, name="codes_" + name, align_bytes=64)
             scales[name] = keep.tile([P, 512], U8, name="scales_" + name, align_bytes=64)
             nc.vector.quantize_mx(out=codes[name][:].bitcast(fmt), scales=scales[name][:], in_=grp[name][:])
 
-        def Q(i, p):
-            name = pairs[i][p]
-            quantize(name, E5M2 if name[0] == "d" else E4M3)
-
-        def DI(name):
-            grp[name] = grpp.tile([P, 2048], BF16, tag="grp", name="grp_" + name, align_bytes=64)
-            o = grp[name][:].rearrange("p (r j) -> p r j", j=4)
-            s = raw[name][:].rearrange("p (j r) -> p r j", j=4)
-            if DOWN_ENGINE[name] == "v":
-                nc.vector.tensor_copy(out=o, in_=s)
-            else:
-                nc.scalar.copy(out=o, in_=s)
-
-        def DQ(name):
-            quantize(name, E4M3)
+        def DI(name, h):
+            if h == 0:
+                grp[name] = dnp.tile([P, 2048], BF16, tag="dgrp", name="grp_" + name, align_bytes=64)
+            cols = slice(h * 256, (h + 1) * 256)
+            o = grp[name][:].rearrange("p (r j) -> p r j", j=4)[:, cols, :]
+            s = raw[name][:].rearrange("p (j r) -> p r j", j=4)[:, cols, :]
+            nc.vector.tensor_copy(out=o, in_=s)
 
         def M(b, tok, q, rank, start, stop):
             if start:
@@ -188,118 +218,81 @@ def tile_stacked_lora_rank_grad_s2_kernel(tc, x, down, dy, up, gate, centre, out
                 stop=stop,
             )
 
-        def O1(b, tile, w):
-            t = resp.tile([P, HALF], F32, tag="res", name="res_%d_%d" % (tile, w))
-            nc.vector.tensor_tensor(out=t[:], in0=acc[b][:], in1=cb[:, w * HALF : (w + 1) * HALF], op=SUB)
-            res[tile, w] = t
+        def O1(b, tile, w, lo=0, hi=HALF):
+            if lo == 0:
+                res[tile, w] = resp.tile([P, HALF], F32, tag="res", name="res_%d_%d" % (tile, w))
+            nc.vector.tensor_tensor(
+                out=res[tile, w][:, lo:hi], in0=acc[b][:, lo:hi], in1=cb[:, w * HALF + lo : w * HALF + hi], op=SUB
+            )
 
-        def O2(tile, w):
+        def O2(tile, w, lo=0, hi=HALF):
             t = res[tile, w]
-            g = gates[tile // 4][:, tile % 4, w * HALF : (w + 1) * HALF]
-            nc.vector.tensor_tensor(out=t[:], in0=t[:], in1=g, op=MULT)
-            nc.sync.dma_start(out=out[tile * P : (tile + 1) * P, w * HALF : (w + 1) * HALF], in_=t[:])
+            g = gates[tile // 4][:, tile % 4, w * HALF + lo : w * HALF + hi]
+            nc.vector.tensor_tensor(out=t[:, lo:hi], in0=t[:, lo:hi], in1=g, op=MULT)
+            nc.sync.dma_start(
+                out=out[tile * P : (tile + 1) * P, w * HALF + lo : w * HALF + hi], in_=t[:, lo:hi]
+            )
 
-        def xq(b):
-            return ("x01" if b < 2 else "x23"), 2 * (b % 2)
+        passes = pass_list()
+        closed = []
+        read = []
+        done = 0
+        ordered = PLAIN_PAIRS
 
-        def token_tile(base, a, parts, first, last):
-            for w in (0, 1):
-                for n, tok in enumerate(parts):
-                    kind = tok[-1] if tok[0] == "d" else "x"
-                    for c in (0, 1):
-                        rank = ("dn%s%d" % ("AB"[w], c)) if kind == "x" else ("up%s%d" % ("AB"[w], c + (2 if kind == "b" else 0)))
-                        M(base + w, tok, 2 * a + c, rank, first and n == 0 and c == 0, last and n == len(parts) - 1 and c == 1)
-
-        def products(i):
-            if 1 <= i <= 4:
-                for b in range(4):
-                    M(b, "dyA%d" % (i - 1), b, "upA%d" % (i - 1), i == 1, False)
-            elif i == 5:
-                for b in range(4):
-                    tok, q = xq(b)
-                    for c in (0, 1):
-                        M(b, tok, q + c, "dnA%d" % c, False, c == 1)
-            elif i == 6:
-                for c in (0, 1):
-                    for b in range(4):
-                        M(b, "dyA%d" % c, b, "upB%d" % c, c == 0, False)
-            elif i == 7:
-                for b in range(4):
-                    for c in (2, 3):
-                        M(b, "dyA%d" % c, b, "upB%d" % c, False, False)
-                    tok, q = xq(b)
-                    for c in (0, 1):
-                        M(b, tok, q + c, "dnB%d" % c, False, c == 1)
-            elif i == 8:
-                token_tile(0, 0, ["dy45a", "dy45b"], True, False)
-            elif i == 9:
-                token_tile(0, 0, ["x45"], False, True)
-                token_tile(2, 1, ["dy45a", "dy45b", "x45"], True, True)
-
-        for j in range(4):
-            R(0, j)
-        for i in range(10):
-            for j in range(4):
-                T(i, j)
-            if i == 6:
-                for b in range(4):
-                    O1(b, b, 0)
-            if i == 8:
-                for b in range(4):
-                    O1(b, b, 1)
-            if i == 0:
+        for p in range(20):
+            T(p, 0)
+            T(p, 1)
+            if p == 0:
                 centre_columns()
-            E(i, 0)
-            R(i + 1, 0)
-            R(i + 1, 1)
-            E(i, 1)
-            Q(i, 0)
-            E(i, 2)
-            R(i + 1, 2)
-            R(i + 1, 3)
-            E(i, 3)
-            Q(i, 1)
-            if i == 0:
+            if p == 1:
                 centre_spread()
-            if i == 3:
-                DI("dnA0")
-            if i == 4:
-                DQ("dnA0")
-                DI("dnA1")
-                DQ("dnA1")
-            if i == 5:
-                DI("dnB0")
-            if i == 6:
-                DI("dnB1")
-                DQ("dnB0")
-                DQ("dnB1")
-            if i == 7:
-                for b in range(4):
-                    O2(b, 0)
-            if i == 8:
-                for b in range(4):
-                    O2(b, 1)
-            products(i)
-            if i == 0:
-                load_tokens("dy45a", dy, 512, 0)
-                load_tokens("dy45b", dy, 512, 1024)
-                load_gate(0)
-            if i == 1:
-                load_tokens("x45", x, 512, 0)
-                load_tokens("dy67a", dy, 768, 0)
-            if i == 2:
-                load_tokens("dy67b", dy, 768, 1024)
-                load_tokens("x67", x, 768, 0)
-                load_gate(1)
-            if i == 9:
-                for tile, b in ((4, 0), (5, 2)):
-                    O1(b, tile, 0)
-                    O1(b + 1, tile, 1)
-                    O2(tile, 0)
-                    O2(tile, 1)
-        for tile, b in ((6, 0), (7, 2)):
-            token_tile(b, tile - 6, ["dy67a", "dy67b", "x67"], True, True)
-            O1(b, tile, 0)
-            O1(b + 1, tile, 1)
-            O2(tile, 0)
-            O2(tile, 1)
+            E(p, 0)
+            E(p, 1)
+            for b, tile, w in closed:
+                O1(b, tile, w)
+                read.append((tile, w))
+            closed = []
+            if p > 0:
+                Q(PAIRS[p - 1])
+            while ordered < 20 and ordered <= p + (1 if p < 7 else 2):
+                R(ordered)
+                ordered += 1
+            for name, at in DOWN_HALVES.items():
+                for h in (0, 1):
+                    if at[h] == p:
+                        DI(name, h)
+            for name, at in DOWN_HALVES.items():
+                if at[1] == p - 1:
+                    Q(name)
+            if p >= 16:
+                for n in range(3):
+                    if read:
+                        O2(*read.pop(0))
+            if p == 5:
+                late_loads()
+            for n in range(PASSES_AFTER[p]):
+                b, tok, q, rank, start, stop, tile, w = passes[done]
+                M(b, tok, q, rank, start, stop)
+                done += 1
+                if stop:
+                    closed.append((b, tile, w))
+        Q(PAIRS[19])
+        for b, tile, w in closed:
+            O1(b, tile, w)
+            read.append((tile, w))
+        for b, tok, q, rank, start, stop, tile, w in passes[done:]:
+            M(b, tok, q, rank, start, stop)
+            if stop:
+                if (tile, w) == (7, 1):
+                    for n in range(len(read)):
+                        O2(*read.pop(0))
+                    O1(b, tile, w, 0, 256)
+                    O1(b, tile, w, 256, 512)
+                    O2(tile, w, 0, 256)
+                    O2(tile, w, 256, 512)
+                else:
+                    O1(b, tile, w)
+                    for n in range(2):
+                        if read and (n == 0 or len(read) > 1):
+                            O2(*read.pop(0))
+                    read.append((tile, w))

@@ -18,48 +18,43 @@ MULT = mybir.AluOpType.mult
 P = 128
 HALF = 512
 
-PASSES_AFTER = (0, 0, 0, 0, 0, 0, 4, 0, 2, 6, 4, 6, 4, 6, 0, 10, 0, 16, 0, 4)
-PLAIN_PAIRS = 7
-VECTOR_PAIRS = 11
-DOWN_HALVES = {"dnA0": (7, 7), "dnA1": (7, 9), "dnB0": (13, 13), "dnB1": (12, 13)}
-
+PASSES_AFTER = (0, 0, 0, 0, 0, 0, 8, 2, 2, 2, 0, 2, 2, 0, 8, 12, 0, 6, 8, 4)
+PLAIN_PAIRS = 13
+SHARED_PAIRS = 15
+DOWN_HALVES = {"dnA0": (7, 7), "dnA1": (9, 9), "dnB0": (10, 13), "dnB1": (9, 11)}
+LEAD_TWO_FROM = 5
+MULTIPLY_FROM = 16
+MULTIPLY_EACH = 4
 
 PAIRS = (
-    "dyA0", "upA0", "dyA1", "upA1", "dyA2", "upA2", "dyA3", "upA3", "x01", "x23",
-    "upB0", "upB1", "upB2", "upB3", "dy45a", "dy45b", "x45", "dy67a", "dy67b", "x67",
+    "upA0", "upA1", "upA2", "upA3", "dy0", "dy1", "dy2", "dy3", "x01", "x23",
+    "upB0", "upB1", "upB2", "upB3", "dy4", "dy5", "x45", "dy6", "dy7", "x67",
 )
+X_OF = ("x01", "x01", "x23", "x23", "x45", "x45", "x67", "x67")
 
 
 def pass_list():
     o = []
 
-    def group_a(w, cs, first):
-        h = "AB"[w]
-        for c in cs:
-            for b in range(4):
-                o.append((b, "dyA%d" % c, b, "up%s%d" % (h, c), first and c == 0, False, b, w))
+    def dy_part(b, t, w):
+        for c in range(4):
+            o.append((b, "dy%d" % t, c, "up%s%d" % ("AB"[w], c), c == 0, False, t, w))
 
-    def x_part(w, b):
-        for c in (0, 1):
-            o.append((b, "x01" if b < 2 else "x23", 2 * (b % 2) + c, "dn%s%d" % ("AB"[w], c), False, c == 1, b, w))
+    def x_part(b, t, w):
+        for c in range(2):
+            o.append((b, X_OF[t], 2 * (t % 2) + c, "dn%s%d" % ("AB"[w], c), False, c == 1, t, w))
 
-    group_a(0, range(4), True)
-    for b in range(4):
-        x_part(0, b)
-    group_a(1, range(2), True)
-    for b in range(4):
-        for c in (2, 3):
-            o.append((b, "dyA%d" % c, b, "upB%d" % c, False, False, b, 1))
-        x_part(1, b)
+    for t in range(4):
+        dy_part(t, t, 0)
+    for t in range(4):
+        x_part(t, t, 0)
+    for t in range(4):
+        dy_part(t, t, 1)
+        x_part(t, t, 1)
     for t in range(4, 8):
-        g = "45" if t < 6 else "67"
-        a = t % 2
-        for w in (0, 1):
-            h = "AB"[w]
-            for c in range(6):
-                tok = ("dy%s%s" % (g, "ab"[c // 2])) if c < 4 else "x" + g
-                rank = ("up%s%d" % (h, c)) if c < 4 else ("dn%s%d" % (h, c - 4))
-                o.append((2 * a + w, tok, 2 * a + c % 2, rank, c == 0, c == 5, t, w))
+        for w in range(2):
+            dy_part(2 * (t % 2) + w, t, w)
+            x_part(2 * (t % 2) + w, t, w)
     return o
 
 
@@ -67,46 +62,48 @@ def tile_stacked_lora_rank_grad_s2_kernel(tc, x, down, dy, up, gate, centre, out
     nc = tc.nc
     with ExitStack() as ctx:
         const = ctx.enter_context(tc.tile_pool(name="const", bufs=1))
-        rawp = ctx.enter_context(tc.tile_pool(name="rawp", bufs=18))
-        rop = ctx.enter_context(tc.tile_pool(name="rop", bufs=8))
+        rawp = ctx.enter_context(tc.tile_pool(name="rawp", bufs=15))
+        rop = ctx.enter_context(tc.tile_pool(name="rop", bufs=6))
+        upgp = ctx.enter_context(tc.tile_pool(name="upgp", bufs=1))
         grpp = ctx.enter_context(tc.tile_pool(name="grpp", bufs=3))
-        dnp = ctx.enter_context(tc.tile_pool(name="dnp", bufs=2))
+        dnp = ctx.enter_context(tc.tile_pool(name="dnp", bufs=3))
         keep = ctx.enter_context(tc.tile_pool(name="keep", bufs=1))
-        resp = ctx.enter_context(tc.tile_pool(name="resp", bufs=12))
+        resp = ctx.enter_context(tc.tile_pool(name="resp", bufs=10))
         psum = ctx.enter_context(tc.psum_pool(name="psum", bufs=1))
         ctx.enter_context(tc.manual_schedule())
 
-        raw, codes, scales, grp, ro, bank = {}, {}, {}, {}, {}, {}
+        raw, rawdn, codes, scales, grp, ro, bank = {}, {}, {}, {}, {}, {}, {}
         acc, res, gates = {}, {}, {}
 
-        def load_cols(name, src, r0, c, split=1):
+        def pair_rows(src, g):
+            return src[256 * g : 256 * (g + 1), :].rearrange("(p a) k -> p a k", a=2)
+
+        def load(name, split=1):
             t = rawp.tile([P, 2048], BF16, tag="raw", name="raw_" + name, align_bytes=64)
-            v = t[:].rearrange("p (a k) -> p a k", a=4)
-            s = src[r0 : r0 + HALF, c * 512 : (c + 1) * 512].rearrange("(a p) k -> p a k", p=P)
-            n = 4 // split
-            for h in range(split):
-                nc.sync.dma_start(out=v[:, h * n : (h + 1) * n, :], in_=s[:, h * n : (h + 1) * n, :])
+            n = int(name[-1])
+            if name[0] == "u":
+                r0 = (0 if name[2] == "A" else 1) * HALF + n * P
+                s = up[r0 : r0 + P, :]
+            elif name[0] == "d":
+                s = pair_rows(dy, n // 2)[:, n % 2, :]
+            else:
+                s = None
+            if s is None:
+                nc.sync.dma_start(out=t[:].rearrange("p (a k) -> p a k", a=2), in_=pair_rows(x, n // 2))
+            else:
+                w = 2048 // split
+                for h in range(split):
+                    nc.sync.dma_start(out=t[:, h * w : (h + 1) * w], in_=s[:, h * w : (h + 1) * w])
             raw[name] = t
 
-        def load_tokens(name, src, r0, k0):
-            t = rawp.tile([P, 2048], BF16, tag="raw", name="raw_" + name, align_bytes=64)
-            nc.sync.dma_start(
-                out=t[:].rearrange("p (a k) -> p a k", a=2),
-                in_=src[r0 : r0 + 256, k0 : k0 + 1024].rearrange("(a p) k -> p a k", p=P),
-            )
-            raw[name] = t
-
-        def load_down(name, c, w):
-            t = rawp.tile([P, 2048], BF16, tag="raw", name="raw_" + name, align_bytes=64)
-            nc.sync.dma_start(
-                out=t[:].rearrange("p (j r) -> p j r", j=4),
-                in_=down[c * 512 : (c + 1) * 512, w * HALF : (w + 1) * HALF].rearrange("(p j) r -> p j r", j=4),
-            )
-            raw[name] = t
+        def load_down(c):
+            t = const.tile([P, 4, RANKS], BF16, name="rawdn_%d" % c, align_bytes=64)
+            nc.sync.dma_start(out=t[:], in_=down[c * 512 : (c + 1) * 512, :].rearrange("(p j) r -> p j r", j=4))
+            rawdn[c] = t
 
         def load_gate(g):
-            t = const.tile([P, 4, RANKS], BF16, name="gate_%d" % g)
-            nc.sync.dma_start(out=t[:], in_=gate[g * HALF : (g + 1) * HALF, :].rearrange("(a p) r -> p a r", p=P))
+            t = const.tile([P, 2, RANKS], BF16, name="gate_%d" % g, align_bytes=64)
+            nc.sync.dma_start(out=t[:], in_=pair_rows(gate, g))
             gates[g] = t
 
         crow = const.tile([P, P], F32, name="crow", align_bytes=64)
@@ -122,29 +119,22 @@ def tile_stacked_lora_rank_grad_s2_kernel(tc, x, down, dy, up, gate, centre, out
         cbw = const.tile([P, HALF], F32, name="cbw", align_bytes=64)
         cb = cbw[:].bitcast(BF16)
 
-        load_cols("dyA0", dy, 0, 0, split=2)
-        load_cols("upA0", up, 0, 0, split=2)
-        for c in (1, 2, 3):
-            load_cols("dyA%d" % c, dy, 0, c)
-            load_cols("upA%d" % c, up, 0, c)
-        load_tokens("x01", x, 0, 0)
-        load_tokens("x23", x, 256, 0)
-        load_down("dnA0", 0, 0)
-        load_down("dnA1", 1, 0)
-        for c in range(4):
-            load_cols("upB%d" % c, up, HALF, c)
-        load_down("dnB0", 0, 1)
-        load_down("dnB1", 1, 1)
+        load("upA0", 2)
+        for name in PAIRS[1:10]:
+            load(name)
+        load_down(0)
+        load_down(1)
+        for name in PAIRS[10:15]:
+            load(name)
 
         def late_loads():
-            load_tokens("dy45a", dy, 512, 0)
-            load_tokens("dy45b", dy, 512, 1024)
+            load("dy5")
             load_gate(0)
-            load_tokens("x45", x, 512, 0)
-            load_tokens("dy67a", dy, 768, 0)
-            load_tokens("dy67b", dy, 768, 1024)
-            load_tokens("x67", x, 768, 0)
             load_gate(1)
+            for name in PAIRS[16:20]:
+                load(name)
+            load_gate(2)
+            load_gate(3)
 
         def centre_columns():
             t = psum.tile([P, HALF], F32, tag="acc0", name="ctr")
@@ -165,7 +155,7 @@ def tile_stacked_lora_rank_grad_s2_kernel(tc, x, down, dy, up, gate, centre, out
                 t = rop.tile([P, 512], F32, tag="ro", name="ro_%d_%d" % (p, j), align_bytes=64)
                 o = t[:].rearrange("p (g u m) -> p g u m", g=2, u=2)
                 s = words(p, j).rearrange("p (g m u) -> p g u m", g=2, u=2)
-                if p < VECTOR_PAIRS:
+                if p < SHARED_PAIRS and j == 0:
                     nc.vector.tensor_copy(out=o, in_=s)
                 else:
                     nc.scalar.copy(out=o, in_=s)
@@ -185,23 +175,40 @@ def tile_stacked_lora_rank_grad_s2_kernel(tc, x, down, dy, up, gate, centre, out
 
         def E(p, j):
             name = PAIRS[p]
-            if j == 0:
-                grp[name] = grpp.tile([P, 2048], BF16, tag="grp", name="grp_" + name, align_bytes=64)
-            o = grp[name][:, j * 1024 : (j + 1) * 1024].bitcast(F32).rearrange("p (g r u) -> p g r u", g=2, u=2)
+            if name[0] == "u":
+                half = name[0:3]
+                rr = int(name[3])
+                if rr == 0 and j == 0:
+                    grp[half] = upgp.tile([P, 8192], BF16, tag="upg", name="grp_" + half, align_bytes=64)
+                o = grp[half][:].bitcast(F32).rearrange("p (c r u) -> p c r u", c=4, u=2)
+                o = o[:, 2 * j : 2 * j + 2, rr * P : (rr + 1) * P, :]
+            else:
+                if j == 0:
+                    grp[name] = grpp.tile([P, 2048], BF16, tag="grp", name="grp_" + name, align_bytes=64)
+                o = grp[name][:, j * 1024 : (j + 1) * 1024].bitcast(F32).rearrange("p (g r u) -> p g r u", g=2, u=2)
             nc.scalar.copy(out=o, in_=bank[p, j][:].rearrange("p (g u r) -> p g r u", g=2, u=2))
 
-        def Q(name):
+        def quantize(name, src):
             fmt = E5M2 if name[0:2] == "dy" else E4M3
             codes[name] = keep.tile([P, 512], U32, name="codes_" + name, align_bytes=64)
             scales[name] = keep.tile([P, 512], U8, name="scales_" + name, align_bytes=64)
-            nc.vector.quantize_mx(out=codes[name][:].bitcast(fmt), scales=scales[name][:], in_=grp[name][:])
+            nc.vector.quantize_mx(out=codes[name][:].bitcast(fmt), scales=scales[name][:], in_=src)
+
+        def Q(p):
+            name = PAIRS[p]
+            if name[0] != "u":
+                quantize(name, grp[name][:])
+            elif name[3] == "3":
+                for c in range(4):
+                    quantize(name[0:3] + str(c), grp[name[0:3]][:, c * 2048 : (c + 1) * 2048])
 
         def DI(name, h):
             if h == 0:
                 grp[name] = dnp.tile([P, 2048], BF16, tag="dgrp", name="grp_" + name, align_bytes=64)
-            cols = slice(h * 256, (h + 1) * 256)
-            o = grp[name][:].rearrange("p (r j) -> p r j", j=4)[:, cols, :]
-            s = raw[name][:].rearrange("p (j r) -> p r j", j=4)[:, cols, :]
+            lo = h * 256
+            col = (0 if name[2] == "A" else 1) * HALF + lo
+            o = grp[name][:].rearrange("p (r j) -> p r j", j=4)[:, lo : lo + 256, :]
+            s = rawdn[int(name[3])][:, :, col : col + 256].rearrange("p j r -> p r j")
             nc.vector.tensor_copy(out=o, in_=s)
 
         def M(b, tok, q, rank, start, stop):
@@ -227,11 +234,9 @@ def tile_stacked_lora_rank_grad_s2_kernel(tc, x, down, dy, up, gate, centre, out
 
         def O2(tile, w, lo=0, hi=HALF):
             t = res[tile, w]
-            g = gates[tile // 4][:, tile % 4, w * HALF + lo : w * HALF + hi]
-            nc.vector.tensor_tensor(out=t[:, lo:hi], in0=t[:, lo:hi], in1=g, op=MULT)
-            nc.sync.dma_start(
-                out=out[tile * P : (tile + 1) * P, w * HALF + lo : w * HALF + hi], in_=t[:, lo:hi]
-            )
+            cols = slice(w * HALF + lo, w * HALF + hi)
+            nc.vector.tensor_tensor(out=t[:, lo:hi], in0=t[:, lo:hi], in1=gates[tile // 2][:, tile % 2, cols], op=MULT)
+            nc.sync.dma_start(out=pair_rows(out, tile // 2)[:, tile % 2, cols], in_=t[:, lo:hi])
 
         passes = pass_list()
         closed = []
@@ -252,20 +257,20 @@ def tile_stacked_lora_rank_grad_s2_kernel(tc, x, down, dy, up, gate, centre, out
                 O1(b, tile, w)
                 read.append((tile, w))
             closed = []
-            if p > 0:
-                Q(PAIRS[p - 1])
-            while ordered < 20 and ordered <= p + (1 if p < 7 else 2):
+            while ordered < 20 and ordered <= p + (1 if p < LEAD_TWO_FROM else 2):
                 R(ordered)
                 ordered += 1
+            if p > 0:
+                Q(p - 1)
             for name, at in DOWN_HALVES.items():
                 for h in (0, 1):
                     if at[h] == p:
                         DI(name, h)
             for name, at in DOWN_HALVES.items():
                 if at[1] == p - 1:
-                    Q(name)
-            if p >= 16:
-                for n in range(3):
+                    quantize(name, grp[name][:])
+            if p >= MULTIPLY_FROM:
+                for n in range(MULTIPLY_EACH):
                     if read:
                         O2(*read.pop(0))
             if p == 5:
@@ -276,7 +281,7 @@ def tile_stacked_lora_rank_grad_s2_kernel(tc, x, down, dy, up, gate, centre, out
                 done += 1
                 if stop:
                     closed.append((b, tile, w))
-        Q(PAIRS[19])
+        Q(19)
         for b, tile, w in closed:
             O1(b, tile, w)
             read.append((tile, w))

@@ -18,42 +18,48 @@ MULT = mybir.AluOpType.mult
 P = 128
 HALF = 512
 
-PASSES_AFTER = (0, 0, 0, 0, 0, 0, 8, 2, 2, 2, 0, 2, 2, 0, 8, 12, 0, 6, 8, 4)
-PLAIN_PAIRS = 13
-SHARED_PAIRS = 15
-DOWN_HALVES = {"dnA0": (7, 7), "dnA1": (9, 9), "dnB0": (10, 13), "dnB1": (9, 11)}
-LEAD_TWO_FROM = 5
+PASSES_AFTER = (0, 0, 0, 0, 4, 0, 0, 0, 0, 2, 9, 0, 4, 0, 7, 19, 0, 12, 0, 4)
+PLAIN_PAIRS = 12
+VECTOR_PAIRS = 16
+ORDER_FIRST_FROM = 12
+DOWN_HALVES = {"dnA0": (8, 9), "dnA1": (10, 10), "dnB0": (8, 8), "dnB1": (10, 13)}
 MULTIPLY_FROM = 16
-MULTIPLY_EACH = 4
+MULTIPLY_EACH = 3
 
 PAIRS = (
-    "upA0", "upA1", "upA2", "upA3", "dy0", "dy1", "dy2", "dy3", "x01", "x23",
-    "upB0", "upB1", "upB2", "upB3", "dy4", "dy5", "x45", "dy6", "dy7", "x67",
+    "dy01a", "U0", "U1", "dy23a", "dy01b", "U2", "U3", "dy23b", "x01", "x23",
+    "uB0", "uB1", "uB2", "uB3", "dy4", "dy5", "x45", "dy6", "dy7", "x67",
 )
+COMPLETES = {"U1": ("upA0", "upA1"), "U3": ("upA2", "upA3"), "uB3": ("upB0", "upB1", "upB2", "upB3")}
 X_OF = ("x01", "x01", "x23", "x23", "x45", "x45", "x67", "x67")
 
 
 def pass_list():
     o = []
 
-    def dy_part(b, t, w):
-        for c in range(4):
-            o.append((b, "dy%d" % t, c, "up%s%d" % ("AB"[w], c), c == 0, False, t, w))
+    def dy_part(b, t, w, cs):
+        for c in cs:
+            if t < 4:
+                tok, q = "dy%s%s" % (("01", "23")[t // 2], "ab"[c // 2]), 2 * (t % 2) + c % 2
+            else:
+                tok, q = "dy%d" % t, c
+            o.append((b, tok, q, "up%s%d" % ("AB"[w], c), c == 0, False, t, w))
 
     def x_part(b, t, w):
         for c in range(2):
             o.append((b, X_OF[t], 2 * (t % 2) + c, "dn%s%d" % ("AB"[w], c), False, c == 1, t, w))
 
-    for t in range(4):
-        dy_part(t, t, 0)
+    for cs in ((0, 1), (2, 3)):
+        for t in range(4):
+            dy_part(t, t, 0, cs)
     for t in range(4):
         x_part(t, t, 0)
     for t in range(4):
-        dy_part(t, t, 1)
+        dy_part(t, t, 1, range(4))
         x_part(t, t, 1)
     for t in range(4, 8):
         for w in range(2):
-            dy_part(2 * (t % 2) + w, t, w)
+            dy_part(2 * (t % 2) + w, t, w, range(4))
             x_part(2 * (t % 2) + w, t, w)
     return o
 
@@ -78,22 +84,29 @@ def tile_stacked_lora_rank_grad_s2_kernel(tc, x, down, dy, up, gate, centre, out
         def pair_rows(src, g):
             return src[256 * g : 256 * (g + 1), :].rearrange("(p a) k -> p a k", a=2)
 
-        def load(name, split=1):
+        def load(name):
             t = rawp.tile([P, 2048], BF16, tag="raw", name="raw_" + name, align_bytes=64)
-            n = int(name[-1])
-            if name[0] == "u":
-                r0 = (0 if name[2] == "A" else 1) * HALF + n * P
-                s = up[r0 : r0 + P, :]
-            elif name[0] == "d":
-                s = pair_rows(dy, n // 2)[:, n % 2, :]
+            two = t[:].rearrange("p (a k) -> p a k", a=2)
+            if name[0] == "x":
+                nc.sync.dma_start(out=two, in_=pair_rows(x, int(name[2]) // 2))
+            elif name[0] == "U":
+                n = int(name[1])
+                rows = up[256 * (n % 2) : 256 * (n % 2) + 256, 1024 * (n // 2) : 1024 * (n // 2) + 1024]
+                nc.sync.dma_start(out=two, in_=rows.rearrange("(a p) k -> p a k", p=P))
+            elif name[0] == "u":
+                r0 = HALF + P * int(name[2])
+                nc.sync.dma_start(out=t[:], in_=up[r0 : r0 + P, :])
+            elif len(name) == 3:
+                n = int(name[2])
+                nc.sync.dma_start(out=t[:], in_=pair_rows(dy, n // 2)[:, n % 2, :])
             else:
-                s = None
-            if s is None:
-                nc.sync.dma_start(out=t[:].rearrange("p (a k) -> p a k", a=2), in_=pair_rows(x, n // 2))
-            else:
-                w = 2048 // split
-                for h in range(split):
-                    nc.sync.dma_start(out=t[:, h * w : (h + 1) * w], in_=s[:, h * w : (h + 1) * w])
+                k0 = 0 if name[4] == "a" else 1024
+                rows = pair_rows(dy, int(name[3]) // 2)[:, :, k0 : k0 + 1024]
+                if name == PAIRS[0]:
+                    nc.sync.dma_start(out=two[:, 0, :], in_=rows[:, 0, :])
+                    nc.sync.dma_start(out=two[:, 1, :], in_=rows[:, 1, :])
+                else:
+                    nc.sync.dma_start(out=two, in_=rows)
             raw[name] = t
 
         def load_down(c):
@@ -119,12 +132,12 @@ def tile_stacked_lora_rank_grad_s2_kernel(tc, x, down, dy, up, gate, centre, out
         cbw = const.tile([P, HALF], F32, name="cbw", align_bytes=64)
         cb = cbw[:].bitcast(BF16)
 
-        load("upA0", 2)
-        for name in PAIRS[1:10]:
+        for name in PAIRS[0:10]:
             load(name)
         load_down(0)
+        load(PAIRS[10])
         load_down(1)
-        for name in PAIRS[10:15]:
+        for name in PAIRS[11:15]:
             load(name)
 
         def late_loads():
@@ -155,7 +168,7 @@ def tile_stacked_lora_rank_grad_s2_kernel(tc, x, down, dy, up, gate, centre, out
                 t = rop.tile([P, 512], F32, tag="ro", name="ro_%d_%d" % (p, j), align_bytes=64)
                 o = t[:].rearrange("p (g u m) -> p g u m", g=2, u=2)
                 s = words(p, j).rearrange("p (g m u) -> p g u m", g=2, u=2)
-                if p < SHARED_PAIRS and j == 0:
+                if p < VECTOR_PAIRS:
                     nc.vector.tensor_copy(out=o, in_=s)
                 else:
                     nc.scalar.copy(out=o, in_=s)
@@ -175,13 +188,15 @@ def tile_stacked_lora_rank_grad_s2_kernel(tc, x, down, dy, up, gate, centre, out
 
         def E(p, j):
             name = PAIRS[p]
-            if name[0] == "u":
-                half = name[0:3]
-                rr = int(name[3])
-                if rr == 0 and j == 0:
+            if name[0] in "uU":
+                if name[0] == "u":
+                    half, rr, c = "upB", int(name[2]), 2 * j
+                else:
+                    half, rr, c = "upA", 2 * (int(name[1]) % 2) + j, 2 * (int(name[1]) // 2)
+                if half not in grp:
                     grp[half] = upgp.tile([P, 8192], BF16, tag="upg", name="grp_" + half, align_bytes=64)
                 o = grp[half][:].bitcast(F32).rearrange("p (c r u) -> p c r u", c=4, u=2)
-                o = o[:, 2 * j : 2 * j + 2, rr * P : (rr + 1) * P, :]
+                o = o[:, c : c + 2, rr * P : (rr + 1) * P, :]
             else:
                 if j == 0:
                     grp[name] = grpp.tile([P, 2048], BF16, tag="grp", name="grp_" + name, align_bytes=64)
@@ -196,11 +211,12 @@ def tile_stacked_lora_rank_grad_s2_kernel(tc, x, down, dy, up, gate, centre, out
 
         def Q(p):
             name = PAIRS[p]
-            if name[0] != "u":
+            if name[0] not in "uU":
                 quantize(name, grp[name][:])
-            elif name[3] == "3":
-                for c in range(4):
-                    quantize(name[0:3] + str(c), grp[name[0:3]][:, c * 2048 : (c + 1) * 2048])
+            elif name in COMPLETES:
+                for rank in COMPLETES[name]:
+                    c = int(rank[3])
+                    quantize(rank, grp[rank[0:3]][:, c * 2048 : (c + 1) * 2048])
 
         def DI(name, h):
             if h == 0:
@@ -209,7 +225,10 @@ def tile_stacked_lora_rank_grad_s2_kernel(tc, x, down, dy, up, gate, centre, out
             col = (0 if name[2] == "A" else 1) * HALF + lo
             o = grp[name][:].rearrange("p (r j) -> p r j", j=4)[:, lo : lo + 256, :]
             s = rawdn[int(name[3])][:, :, col : col + 256].rearrange("p j r -> p r j")
-            nc.vector.tensor_copy(out=o, in_=s)
+            if h == 0:
+                nc.vector.tensor_copy(out=o, in_=s)
+            else:
+                nc.scalar.copy(out=o, in_=s)
 
         def M(b, tok, q, rank, start, stop):
             if start:
@@ -242,7 +261,6 @@ def tile_stacked_lora_rank_grad_s2_kernel(tc, x, down, dy, up, gate, centre, out
         closed = []
         read = []
         done = 0
-        ordered = PLAIN_PAIRS
 
         for p in range(20):
             T(p, 0)
@@ -251,15 +269,16 @@ def tile_stacked_lora_rank_grad_s2_kernel(tc, x, down, dy, up, gate, centre, out
                 centre_columns()
             if p == 1:
                 centre_spread()
+            if p + 1 >= PLAIN_PAIRS and p >= ORDER_FIRST_FROM and p < 19:
+                R(p + 1)
             E(p, 0)
             E(p, 1)
             for b, tile, w in closed:
                 O1(b, tile, w)
                 read.append((tile, w))
             closed = []
-            while ordered < 20 and ordered <= p + (1 if p < LEAD_TWO_FROM else 2):
-                R(ordered)
-                ordered += 1
+            if p + 1 >= PLAIN_PAIRS and p < ORDER_FIRST_FROM:
+                R(p + 1)
             if p > 0:
                 Q(p - 1)
             for name, at in DOWN_HALVES.items():

from contextlib import ExitStack

import concourse.mybir as mybir
from concourse.masks import make_identity

TOKENS, FEATURES, OUT_FEATURES, RANKS = 1024, 1024, 2048, 1024
FLOPS = 2 * TOKENS * RANKS * (FEATURES + OUT_FEATURES)

F32 = mybir.dt.float32
BF16 = mybir.dt.bfloat16
U32 = mybir.dt.uint32
U8 = mybir.dt.uint8
E4M3 = mybir.dt.float8_e4m3fn_x4
E5M2 = mybir.dt.float8_e5m2_x4
SUB = mybir.AluOpType.subtract
MULT = mybir.AluOpType.mult

P = 128
HALF = 512

PASSES_AFTER = (0, 0, 0, 0, 4, 0, 0, 0, 0, 2, 9, 0, 4, 0, 7, 19, 0, 12, 0, 4)
PLAIN_PAIRS = 12
VECTOR_PAIRS = 16
ORDER_FIRST_FROM = 12
DOWN_HALVES = {"dnA0": (8, 9), "dnA1": (10, 10), "dnB0": (8, 8), "dnB1": (10, 13)}
MULTIPLY_FROM = 16
MULTIPLY_EACH = 3

PAIRS = (
    "dy01a", "U0", "U1", "dy23a", "dy01b", "U2", "U3", "dy23b", "x01", "x23",
    "uB0", "uB1", "uB2", "uB3", "dy4", "dy5", "x45", "dy6", "dy7", "x67",
)
COMPLETES = {"U1": ("upA0", "upA1"), "U3": ("upA2", "upA3"), "uB3": ("upB0", "upB1", "upB2", "upB3")}
X_OF = ("x01", "x01", "x23", "x23", "x45", "x45", "x67", "x67")


def pass_list():
    o = []

    def dy_part(b, t, w, cs):
        for c in cs:
            if t < 4:
                tok, q = "dy%s%s" % (("01", "23")[t // 2], "ab"[c // 2]), 2 * (t % 2) + c % 2
            else:
                tok, q = "dy%d" % t, c
            o.append((b, tok, q, "up%s%d" % ("AB"[w], c), c == 0, False, t, w))

    def x_part(b, t, w):
        for c in range(2):
            o.append((b, X_OF[t], 2 * (t % 2) + c, "dn%s%d" % ("AB"[w], c), False, c == 1, t, w))

    for cs in ((0, 1), (2, 3)):
        for t in range(4):
            dy_part(t, t, 0, cs)
    for t in range(4):
        x_part(t, t, 0)
    for t in range(4):
        dy_part(t, t, 1, range(4))
        x_part(t, t, 1)
    for t in range(4, 8):
        for w in range(2):
            dy_part(2 * (t % 2) + w, t, w, range(4))
            x_part(2 * (t % 2) + w, t, w)
    return o


def tile_stacked_lora_rank_grad_s2_kernel(tc, x, down, dy, up, gate, centre, out):
    nc = tc.nc
    with ExitStack() as ctx:
        const = ctx.enter_context(tc.tile_pool(name="const", bufs=1))
        rawp = ctx.enter_context(tc.tile_pool(name="rawp", bufs=15))
        rop = ctx.enter_context(tc.tile_pool(name="rop", bufs=6))
        upgp = ctx.enter_context(tc.tile_pool(name="upgp", bufs=1))
        grpp = ctx.enter_context(tc.tile_pool(name="grpp", bufs=3))
        dnp = ctx.enter_context(tc.tile_pool(name="dnp", bufs=3))
        keep = ctx.enter_context(tc.tile_pool(name="keep", bufs=1))
        resp = ctx.enter_context(tc.tile_pool(name="resp", bufs=10))
        psum = ctx.enter_context(tc.psum_pool(name="psum", bufs=1))
        ctx.enter_context(tc.manual_schedule())

        raw, rawdn, codes, scales, grp, ro, bank = {}, {}, {}, {}, {}, {}, {}
        acc, res, gates = {}, {}, {}

        def pair_rows(src, g):
            return src[256 * g : 256 * (g + 1), :].rearrange("(p a) k -> p a k", a=2)

        def load(name):
            t = rawp.tile([P, 2048], BF16, tag="raw", name="raw_" + name, align_bytes=64)
            two = t[:].rearrange("p (a k) -> p a k", a=2)
            if name[0] == "x":
                nc.sync.dma_start(out=two, in_=pair_rows(x, int(name[2]) // 2))
            elif name[0] == "U":
                n = int(name[1])
                rows = up[256 * (n % 2) : 256 * (n % 2) + 256, 1024 * (n // 2) : 1024 * (n // 2) + 1024]
                nc.sync.dma_start(out=two, in_=rows.rearrange("(a p) k -> p a k", p=P))
            elif name[0] == "u":
                r0 = HALF + P * int(name[2])
                nc.sync.dma_start(out=t[:], in_=up[r0 : r0 + P, :])
            elif len(name) == 3:
                n = int(name[2])
                nc.sync.dma_start(out=t[:], in_=pair_rows(dy, n // 2)[:, n % 2, :])
            else:
                k0 = 0 if name[4] == "a" else 1024
                rows = pair_rows(dy, int(name[3]) // 2)[:, :, k0 : k0 + 1024]
                if name == PAIRS[0]:
                    nc.sync.dma_start(out=two[:, 0, :], in_=rows[:, 0, :])
                    nc.sync.dma_start(out=two[:, 1, :], in_=rows[:, 1, :])
                else:
                    nc.sync.dma_start(out=two, in_=rows)
            raw[name] = t

        def load_down(c):
            t = const.tile([P, 4, RANKS], BF16, name="rawdn_%d" % c, align_bytes=64)
            nc.sync.dma_start(out=t[:], in_=down[c * 512 : (c + 1) * 512, :].rearrange("(p j) r -> p j r", j=4))
            rawdn[c] = t

        def load_gate(g):
            t = const.tile([P, 2, RANKS], BF16, name="gate_%d" % g, align_bytes=64)
            nc.sync.dma_start(out=t[:], in_=pair_rows(gate, g))
            gates[g] = t

        crow = const.tile([P, P], F32, name="crow", align_bytes=64)
        nc.vector.memset(crow[:], 0.0)
        nc.scalar.dma_start(out=crow[0:4, :].bitcast(BF16), in_=centre.rearrange("(m q) -> m q", m=4))
        dummy = const.tile([P, 8], F32, name="dummy")
        nc.vector.memset(dummy[:], 0.0)
        dummy2 = const.tile([P, 8], F32, name="dummy2")
        nc.scalar.copy(out=dummy2[:], in_=dummy[:])
        ident = const.tile([P, P], F32, name="ident", align_bytes=64)
        make_identity(nc, ident[:])
        c4 = const.tile([P, 4], F32, name="c4")
        cbw = const.tile([P, HALF], F32, name="cbw", align_bytes=64)
        cb = cbw[:].bitcast(BF16)

        for name in PAIRS[0:10]:
            load(name)
        load_down(0)
        load(PAIRS[10])
        load_down(1)
        for name in PAIRS[11:15]:
            load(name)

        def late_loads():
            load("dy5")
            load_gate(0)
            load_gate(1)
            for name in PAIRS[16:20]:
                load(name)
            load_gate(2)
            load_gate(3)

        def centre_columns():
            t = psum.tile([P, HALF], F32, tag="acc0", name="ctr")
            nc.tensor.transpose(t[:, 0:P], crow[:], ident[:])
            nc.vector.tensor_copy(out=c4[:], in_=t[:, 0:4])

        def centre_spread():
            t = psum.tile([P, HALF], F32, tag="acc1", name="ctrb")
            for m in range(4):
                nc.tensor.transpose(t[:, m * P : (m + 1) * P], c4[:, m : m + 1].to_broadcast([P, P]), ident[:])
            nc.vector.tensor_copy(out=cbw[:], in_=t[:])

        def words(p, j):
            return raw[PAIRS[p]][:, j * 1024 : (j + 1) * 1024].bitcast(F32)

        def R(p):
            for j in (0, 1):
                t = rop.tile([P, 512], F32, tag="ro", name="ro_%d_%d" % (p, j), align_bytes=64)
                o = t[:].rearrange("p (g u m) -> p g u m", g=2, u=2)
                s = words(p, j).rearrange("p (g m u) -> p g u m", g=2, u=2)
                if p < VECTOR_PAIRS:
                    nc.vector.tensor_copy(out=o, in_=s)
                else:
                    nc.scalar.copy(out=o, in_=s)
                ro[p, j] = t

        def T(p, j):
            b = psum.tile([P, 512], F32, tag="t%d" % (2 * (p % 2) + j), name="tb_%d_%d" % (p, j))
            for g in range(2):
                for u in range(2):
                    q = 2 * g + u
                    if p < PLAIN_PAIRS:
                        src = words(p, j)[:, 256 * g + u : 256 * (g + 1) : 2]
                    else:
                        src = ro[p, j][:, q * P : (q + 1) * P]
                    nc.tensor.transpose(b[:, q * P : (q + 1) * P], src, ident[:])
            bank[p, j] = b

        def E(p, j):
            name = PAIRS[p]
            if name[0] in "uU":
                if name[0] == "u":
                    half, rr, c = "upB", int(name[2]), 2 * j
                else:
                    half, rr, c = "upA", 2 * (int(name[1]) % 2) + j, 2 * (int(name[1]) // 2)
                if half not in grp:
                    grp[half] = upgp.tile([P, 8192], BF16, tag="upg", name="grp_" + half, align_bytes=64)
                o = grp[half][:].bitcast(F32).rearrange("p (c r u) -> p c r u", c=4, u=2)
                o = o[:, c : c + 2, rr * P : (rr + 1) * P, :]
            else:
                if j == 0:
                    grp[name] = grpp.tile([P, 2048], BF16, tag="grp", name="grp_" + name, align_bytes=64)
                o = grp[name][:, j * 1024 : (j + 1) * 1024].bitcast(F32).rearrange("p (g r u) -> p g r u", g=2, u=2)
            nc.scalar.copy(out=o, in_=bank[p, j][:].rearrange("p (g u r) -> p g r u", g=2, u=2))

        def quantize(name, src):
            fmt = E5M2 if name[0:2] == "dy" else E4M3
            codes[name] = keep.tile([P, 512], U32, name="codes_" + name, align_bytes=64)
            scales[name] = keep.tile([P, 512], U8, name="scales_" + name, align_bytes=64)
            nc.vector.quantize_mx(out=codes[name][:].bitcast(fmt), scales=scales[name][:], in_=src)

        def Q(p):
            name = PAIRS[p]
            if name[0] not in "uU":
                quantize(name, grp[name][:])
            elif name in COMPLETES:
                for rank in COMPLETES[name]:
                    c = int(rank[3])
                    quantize(rank, grp[rank[0:3]][:, c * 2048 : (c + 1) * 2048])

        def DI(name, h):
            if h == 0:
                grp[name] = dnp.tile([P, 2048], BF16, tag="dgrp", name="grp_" + name, align_bytes=64)
            lo = h * 256
            col = (0 if name[2] == "A" else 1) * HALF + lo
            o = grp[name][:].rearrange("p (r j) -> p r j", j=4)[:, lo : lo + 256, :]
            s = rawdn[int(name[3])][:, :, col : col + 256].rearrange("p j r -> p r j")
            if h == 0:
                nc.vector.tensor_copy(out=o, in_=s)
            else:
                nc.scalar.copy(out=o, in_=s)

        def M(b, tok, q, rank, start, stop):
            if start:
                acc[b] = psum.tile([P, HALF], F32, tag="acc%d" % b, name="acc_%d" % b)
            cols = slice(q * P, (q + 1) * P)
            nc.tensor.matmul_mx(
                out=acc[b][:],
                lhsT=codes[tok][:, cols].bitcast(E5M2 if tok[0] == "d" else E4M3),
                lhsT_scale=scales[tok][:, cols],
                rhs=codes[rank][:].bitcast(E4M3),
                rhs_scale=scales[rank][:],
                start=start,
                stop=stop,
            )

        def O1(b, tile, w, lo=0, hi=HALF):
            if lo == 0:
                res[tile, w] = resp.tile([P, HALF], F32, tag="res", name="res_%d_%d" % (tile, w))
            nc.vector.tensor_tensor(
                out=res[tile, w][:, lo:hi], in0=acc[b][:, lo:hi], in1=cb[:, w * HALF + lo : w * HALF + hi], op=SUB
            )

        def O2(tile, w, lo=0, hi=HALF):
            t = res[tile, w]
            cols = slice(w * HALF + lo, w * HALF + hi)
            nc.vector.tensor_tensor(out=t[:, lo:hi], in0=t[:, lo:hi], in1=gates[tile // 2][:, tile % 2, cols], op=MULT)
            nc.sync.dma_start(out=pair_rows(out, tile // 2)[:, tile % 2, cols], in_=t[:, lo:hi])

        passes = pass_list()
        closed = []
        read = []
        done = 0

        for p in range(20):
            T(p, 0)
            T(p, 1)
            if p == 0:
                centre_columns()
            if p == 1:
                centre_spread()
            if p + 1 >= PLAIN_PAIRS and p >= ORDER_FIRST_FROM and p < 19:
                R(p + 1)
            E(p, 0)
            E(p, 1)
            for b, tile, w in closed:
                O1(b, tile, w)
                read.append((tile, w))
            closed = []
            if p + 1 >= PLAIN_PAIRS and p < ORDER_FIRST_FROM:
                R(p + 1)
            if p > 0:
                Q(p - 1)
            for name, at in DOWN_HALVES.items():
                for h in (0, 1):
                    if at[h] == p:
                        DI(name, h)
            for name, at in DOWN_HALVES.items():
                if at[1] == p - 1:
                    quantize(name, grp[name][:])
            if p >= MULTIPLY_FROM:
                for n in range(MULTIPLY_EACH):
                    if read:
                        O2(*read.pop(0))
            if p == 5:
                late_loads()
            for n in range(PASSES_AFTER[p]):
                b, tok, q, rank, start, stop, tile, w = passes[done]
                M(b, tok, q, rank, start, stop)
                done += 1
                if stop:
                    closed.append((b, tile, w))
        Q(19)
        for b, tile, w in closed:
            O1(b, tile, w)
            read.append((tile, w))
        for b, tok, q, rank, start, stop, tile, w in passes[done:]:
            M(b, tok, q, rank, start, stop)
            if stop:
                if (tile, w) == (7, 1):
                    for n in range(len(read)):
                        O2(*read.pop(0))
                    O1(b, tile, w, 0, 256)
                    O1(b, tile, w, 256, 512)
                    O2(tile, w, 0, 256)
                    O2(tile, w, 256, 512)
                else:
                    O1(b, tile, w)
                    for n in range(2):
                        if read and (n == 0 or len(read) > 1):
                            O2(*read.pop(0))
                    read.append((tile, w))
